import numpy as np
CORES = [5,13,21,29,37,45,53,61,197,205,213,221,229,237,245,253]
N = 16
def setup_inputs(rng):
    return {"x": rng.standard_normal((N, 128, 256), dtype=np.float32)}
def reference(x):
    s = x.sum(axis=0, dtype=np.float64).astype(x.dtype)
    return {"y": np.broadcast_to(s, (N,) + s.shape)}

@@ -1,0 +1,60 @@
+from concourse.bass import DstId, RemoteDMATransfer
+
+HELPERS = (2, 3)
+NH = len(HELPERS)
+W = 32 // NH
+NP = 8
+
+SCRATCH = {
+    "pieces": ("dram", [NP * NH, 128, W], "float32"),
+    "res": ("dram", [NP * NH, 128, W], "float32"),
+    "part": ("dram", [128, W], "float32"),
+}
+SEMAPHORES = ["local", "sent", "arrived", "mate", "done"]
+
+
+def core_of(chip, k):
+    return (chip // 8) * 128 + chip * 8 + k
+
+
+def rank_program(g, core, T, topo):
+    chip, k = topo.chip(core), core % 8
+    if topo.host(core) != chip // 8:
+        return
+    pair, par = chip // 2, chip % 2
+
+    def dst_id(d):
+        rid, pid = topo.addr(d, core)
+        return DstId(rid=rid, pnc=pid)
+
+    if T.rank_of(core) is not None:
+        g.dma_start(T.pieces[:], T.x[:]).then_inc(T.sem.local, 16)
+        g.wait_ge(T.sem.local, 16)
+        for h in range(NH):
+            g.remote_dma_fused(
+                [RemoteDMATransfer(dst_ids=[dst_id(core_of(2 * q + par, HELPERS[h]))], dma_engine_mask=1 << q,
+                                   remote_sem=T.sem.arrived, src=T.pieces[q * NH + h], dst=T.pieces[pair])
+                 for q in range(NP)],
+                local_sem=T.sem.sent)
+        g.wait_ge(T.sem.done, NP * NH * 8)
+        g.dma_start(T.y[:], T.res[:]).then_inc(T.sem.local, 16)
+        g.wait_ge(T.sem.local, 32)
+        g.wait_ge(T.sem.sent, NP * NH)
+        return
+
+    if k not in HELPERS:
+        return
+    h = HELPERS.index(k)
+    copies = [T.pieces[i] for i in range(NP)]
+    g.wait_ge(T.sem.arrived, NP)
+    g.remote_dma_fused(
+        [RemoteDMATransfer(dst_ids=[dst_id(core_of(chip ^ 1, k))], dma_engine_mask=0xFF, remote_sem=T.sem.mate,
+                           srcs=copies, dsts=[T.part[:]], alu_op=1)],
+        local_sem=T.sem.sent)
+    g.wait_ge(T.sem.mate, 8)
+    g.remote_dma_fused(
+        [RemoteDMATransfer(dst_ids=[dst_id(core_of(2 * q + par, 5)) for q in range(NP)], dma_engine_mask=0xFF,
+                           remote_sem=T.sem.done, srcs=copies + [T.part[:]],
+                           dsts=[T.res[pair * NH + h] for q in range(NP)], alu_op=1)],
+        local_sem=T.sem.sent)
+    g.wait_ge(T.sem.sent, 16)

@@ -1,16 +1,14 @@
 from concourse.bass import DstId, RemoteDMATransfer
 
+RANK_CORE = 5
 HELPERS = (2, 3)
-NH = len(HELPERS)
-W = 32 // NH
 NP = 8
+PART = NP
 
 SCRATCH = {
-    "pieces": ("dram", [NP * NH, 128, W], "float32"),
-    "res": ("dram", [NP * NH, 128, W], "float32"),
-    "part": ("dram", [128, W], "float32"),
+    "buf": ("dram", [2 * NP, 128, 16], "float32"),
 }
-SEMAPHORES = ["local", "sent", "arrived", "mate", "done"]
+SEMAPHORES = ["load0", "load1", "done0", "done1", "stored", "sent", "arrived", "mate"]
 
 
 def core_of(chip, k):
@@ -27,34 +25,39 @@ def rank_program(g, core, T, topo):
         rid, pid = topo.addr(d, core)
         return DstId(rid=rid, pnc=pid)
 
-    if T.rank_of(core) is not None:
-        g.dma_start(T.pieces[:], T.x[:]).then_inc(T.sem.local, 16)
-        g.wait_ge(T.sem.local, 16)
-        for h in range(NH):
+    if k == RANK_CORE:
+        queues = (g.sync, g.scalar)
+        load = (T.sem.load0, T.sem.load1)
+        done = (T.sem.done0, T.sem.done1)
+        for h in range(2):
+            queues[h].dma_start(T.buf[NP * h:NP * (h + 1)], T.x[64 * h:64 * (h + 1), :]).then_inc(load[h], 16)
+        for h in range(2):
+            g.wait_ge(load[h], 16)
             g.remote_dma_fused(
                 [RemoteDMATransfer(dst_ids=[dst_id(core_of(2 * q + par, HELPERS[h]))], dma_engine_mask=1 << q,
-                                   remote_sem=T.sem.arrived, src=T.pieces[q * NH + h], dst=T.pieces[pair])
+                                   remote_sem=T.sem.arrived, src=T.buf[NP * h + q], dst=T.buf[pair])
                  for q in range(NP)],
                 local_sem=T.sem.sent)
-        g.wait_ge(T.sem.done, NP * NH * 8)
-        g.dma_start(T.y[:], T.res[:]).then_inc(T.sem.local, 16)
-        g.wait_ge(T.sem.local, 32)
-        g.wait_ge(T.sem.sent, NP * NH)
+        for h in range(2):
+            queues[h].wait_ge(done[h], NP * 8)
+            queues[h].dma_start(T.y[64 * h:64 * (h + 1), :], T.buf[NP * h:NP * (h + 1)]).then_inc(T.sem.stored, 16)
+        g.wait_ge(T.sem.sent, 2 * NP)
+        g.wait_ge(T.sem.stored, 32)
         return
 
     if k not in HELPERS:
         return
     h = HELPERS.index(k)
-    copies = [T.pieces[i] for i in range(NP)]
+    copies = [T.buf[i] for i in range(NP)]
     g.wait_ge(T.sem.arrived, NP)
     g.remote_dma_fused(
         [RemoteDMATransfer(dst_ids=[dst_id(core_of(chip ^ 1, k))], dma_engine_mask=0xFF, remote_sem=T.sem.mate,
-                           srcs=copies, dsts=[T.part[:]], alu_op=1)],
+                           srcs=copies, dsts=[T.buf[PART]], alu_op=1)],
         local_sem=T.sem.sent)
     g.wait_ge(T.sem.mate, 8)
     g.remote_dma_fused(
-        [RemoteDMATransfer(dst_ids=[dst_id(core_of(2 * q + par, 5)) for q in range(NP)], dma_engine_mask=0xFF,
-                           remote_sem=T.sem.done, srcs=copies + [T.part[:]],
-                           dsts=[T.res[pair * NH + h] for q in range(NP)], alu_op=1)],
+        [RemoteDMATransfer(dst_ids=[dst_id(core_of(2 * q + par, RANK_CORE)) for q in range(NP)], dma_engine_mask=0xFF,
+                           remote_sem=(T.sem.done0, T.sem.done1)[h], srcs=copies + [T.buf[PART]],
+                           dsts=[T.buf[NP * h + pair] for q in range(NP)], alu_op=1)],
         local_sem=T.sem.sent)
     g.wait_ge(T.sem.sent, 16)

from concourse.bass import DstId, RemoteDMATransfer

RANK_CORE = 5
HELPERS = (2, 3)
NP = 8
PART = NP

SCRATCH = {
    "buf": ("dram", [2 * NP, 128, 16], "float32"),
}
SEMAPHORES = ["load0", "load1", "done0", "done1", "stored", "sent", "arrived", "mate"]


def core_of(chip, k):
    return (chip // 8) * 128 + chip * 8 + k


def rank_program(g, core, T, topo):
    chip, k = topo.chip(core), core % 8
    if topo.host(core) != chip // 8:
        return
    pair, par = chip // 2, chip % 2

    def dst_id(d):
        rid, pid = topo.addr(d, core)
        return DstId(rid=rid, pnc=pid)

    if k == RANK_CORE:
        queues = (g.sync, g.scalar)
        load = (T.sem.load0, T.sem.load1)
        done = (T.sem.done0, T.sem.done1)
        for h in range(2):
            queues[h].dma_start(T.buf[NP * h:NP * (h + 1)], T.x[64 * h:64 * (h + 1), :]).then_inc(load[h], 16)
        for h in range(2):
            g.wait_ge(load[h], 16)
            g.remote_dma_fused(
                [RemoteDMATransfer(dst_ids=[dst_id(core_of(2 * q + par, HELPERS[h]))], dma_engine_mask=1 << q,
                                   remote_sem=T.sem.arrived, src=T.buf[NP * h + q], dst=T.buf[pair])
                 for q in range(NP)],
                local_sem=T.sem.sent)
        for h in range(2):
            queues[h].wait_ge(done[h], NP * 8)
            queues[h].dma_start(T.y[64 * h:64 * (h + 1), :], T.buf[NP * h:NP * (h + 1)]).then_inc(T.sem.stored, 16)
        g.wait_ge(T.sem.sent, 2 * NP)
        g.wait_ge(T.sem.stored, 32)
        return

    if k not in HELPERS:
        return
    h = HELPERS.index(k)
    copies = [T.buf[i] for i in range(NP)]
    g.wait_ge(T.sem.arrived, NP)
    g.remote_dma_fused(
        [RemoteDMATransfer(dst_ids=[dst_id(core_of(chip ^ 1, k))], dma_engine_mask=0xFF, remote_sem=T.sem.mate,
                           srcs=copies, dsts=[T.buf[PART]], alu_op=1)],
        local_sem=T.sem.sent)
    g.wait_ge(T.sem.mate, 8)
    g.remote_dma_fused(
        [RemoteDMATransfer(dst_ids=[dst_id(core_of(2 * q + par, RANK_CORE)) for q in range(NP)], dma_engine_mask=0xFF,
                           remote_sem=(T.sem.done0, T.sem.done1)[h], srcs=copies + [T.buf[PART]],
                           dsts=[T.buf[NP * h + pair] for q in range(NP)], alu_op=1)],
        local_sem=T.sem.sent)
    g.wait_ge(T.sem.sent, 16)
